import numpy as np
import ml_dtypes


def mxq(x, axis, fmt="e4m3"):
    dtype, down = {"e4m3": (ml_dtypes.float8_e4m3fn, 7), "e5m2": (ml_dtypes.float8_e5m2, 14)}[fmt]
    v = np.moveaxis(np.asarray(x, np.float32).astype(ml_dtypes.bfloat16).astype(np.float64), axis, -1)
    blocks = v.reshape(v.shape[:-1] + (-1, 32))
    amax = np.abs(blocks).max(-1, keepdims=True)
    byte = np.maximum(np.where(amax > 0, np.frexp(amax)[1] - 1 + 127, 0) - down, 1)
    scale = np.exp2(byte - 127.0)
    codes = (blocks / scale).astype(np.float32).astype(dtype).astype(np.float64)
    return np.moveaxis((codes * scale).reshape(v.shape), -1, axis)


WIDE = False


def mx_kscale(k):
    if not WIDE:
        return np.ones(k)
    levels = np.array([10, -10, 5, -5, 0])
    if k % 512:
        return np.exp2(np.random.permutation(np.resize(levels, k // 32))).repeat(32)
    a = np.empty((k // 512, 16))
    for p in range(k // 512):
        a[p, :8] = np.random.permutation(np.resize(levels, 8))
        for g in range(8):
            far = levels[np.abs(levels - a[p, g]) >= 10]
            a[p, g + 8] = far[np.random.randint(len(far))]
    return np.exp2(a.ravel()).repeat(32)


def f64(x):
    return np.asarray(x).astype(np.float64)


def striped(idx):
    return np.tile(np.asarray(idx).reshape(-1, 16).T, (8, 1)).astype(np.uint16)


def unstriped(offs):
    return offs[:16].T.reshape(-1).astype(np.int64)


E2M1 = np.array([0.0, 0.5, 1.0, 1.5, 2.0, 3.0, 4.0, 6.0, -0.0, -0.5, -1.0, -1.5, -2.0, -3.0, -4.0, -6.0])


def pack_weight(w, fmt):
    k, n = w.shape
    w = f64(np.asarray(w, np.float32).astype(ml_dtypes.bfloat16)).reshape(k // 32, 32, n)
    amax = np.abs(w).max(1)
    if fmt == "e4m3":
        byte = np.frexp(amax)[1] - 1 + 127 - 7
    else:
        mant, ex = np.frexp(amax / 6.0)
        byte = np.where(mant > 0.5, ex, ex - 1) + 127
    byte = np.clip(np.where(amax > 0, byte, 1), 1, 254)
    scaled = (w * np.exp2(127.0 - byte)[:, None, :]).reshape(k, n).astype(np.float32)
    by_word = np.ascontiguousarray(scaled.reshape(k // 512, 128, 4, n).transpose(0, 1, 3, 2))
    if fmt == "e4m3":
        words = by_word.astype(ml_dtypes.float8_e4m3fn).view(np.uint8)
    else:
        c = by_word.astype(ml_dtypes.float4_e2m1fn).view(np.uint8) & 0xF
        words = (c[..., 0::2] | (c[..., 1::2] << 4)).reshape(k // 512, 128, 2 * n)
    return np.ascontiguousarray(words), np.ascontiguousarray(byte.astype(np.uint8).reshape(k // 512, 16, n))


def unpack_weight(words, scales, fmt):
    g, _, n = scales.shape
    words = np.ascontiguousarray(words).reshape(g, 128, n, -1)
    if fmt == "e4m3":
        vals = words.view(ml_dtypes.float8_e4m3fn).astype(np.float64)
    else:
        nib = np.empty((g, 128, n, 4), np.uint8)
        nib[..., 0::2] = words & 0xF
        nib[..., 1::2] = words >> 4
        vals = E2M1[nib]
    vals = vals * np.repeat(np.exp2(scales.astype(np.float64) - 127.0), 8, axis=1)[..., None]
    return vals.transpose(0, 1, 3, 2).reshape(g * 512, n)


def softplus(v):
    return np.log(1.0 + np.exp(v))


D, T, I, Q = 512, 2048, 512, 128


def setup_inputs():
    n = np.random.standard_normal
    idx = np.random.permutation(T)[:I]
    fd = mx_kscale(D)
    keysp = pack_weight(n((D, T)) / fd[:, None], "e4m3")
    return {
        "query": (n((D, Q)) * 1.0 / np.sqrt(D) * fd[:, None]).astype(np.float32),
        "keys_words": keysp[0],
        "keys_scales": keysp[1],
        "margin": (np.random.uniform(0.0, 0.5, (1, I))).astype(np.float32),
        "steep": (np.random.uniform(0.5, 2.0, (Q, 1))).astype(np.float32),
        "offs": striped(idx),
    }


def reference(query, keys_words, keys_scales, margin, steep, offs):
    idx = unstriped(offs)
    keysu = unpack_weight(keys_words, keys_scales, "e4m3")
    queryq = mxq(f64(query), 0, "e4m3")
    keysidxg = keysu[:, idx]
    a = queryq.T @ keysidxg
    b = np.pad(a, ((0, 0), (1, 0)))[:, :I]
    y = softplus((a - b + f64(margin)) * f64(steep))
    return y

@@ -1,0 +1,120 @@
+from contextlib import ExitStack
+
+import concourse.mybir as mybir
+
+D, T, I, Q = 512, 2048, 512, 128
+FLOPS = 2 * D * I * Q
+
+F32 = mybir.dt.float32
+BF16 = mybir.dt.bfloat16
+I32 = mybir.dt.int32
+U32 = mybir.dt.uint32
+U16 = mybir.dt.uint16
+U8 = mybir.dt.uint8
+FP8X4 = mybir.dt.float8_e4m3fn_x4
+ALU = mybir.AluOpType
+ACT = mybir.ActivationFunctionType
+
+P = 128
+PACK = 4
+HALF = I // 2
+
+
+def tile_attend_rankgaps_kernel(tc, query, keys_words, keys_scales, margin, steep, offs, out):
+    nc = tc.nc
+    with ExitStack() as ctx:
+        sb = ctx.enter_context(tc.tile_pool(name="sb", bufs=1))
+        ps = ctx.enter_context(tc.psum_pool(name="ps", bufs=1))
+
+        offsets = sb.tile([P, I // 16], U16, name="offsets")
+        q_raw = sb.tile([P, PACK, Q], F32, name="q_raw")
+        words = sb.tile([P, T], I32, name="words", align_bytes=64)
+        scales = sb.tile([P, T], U8, name="scales", align_bytes=64)
+        m_cols = sb.tile([P, PACK], F32, name="m_cols")
+        half = sb.tile([P, 1], F32, name="half")
+        warm = sb.tile([P, 1], F32, name="warm")
+
+        nc.vector.memset(scales[:].bitcast(I32), 0)
+        nc.vector.memset(half[:], 0.5)
+
+        nc.sync.dma_start(offsets[:], offs)
+        nc.sync.dma_start(q_raw[:], query.rearrange("(p j) q -> p j q", j=PACK))
+        nc.scalar.dma_start(m_cols[:], margin.rearrange("o (p j) -> (o p) j", j=PACK))
+        for quad in range(4):
+            nc.sync.dma_start(
+                scales[32 * quad : 32 * quad + 4, :].bitcast(I32),
+                keys_scales[0][4 * quad : 4 * quad + 4, :].bitcast(I32),
+            )
+        nc.sync.dma_start(words[:], keys_words[0].rearrange("p n t -> p (n t)").bitcast(I32))
+        nc.scalar.activation(warm[:], half[:], ACT.Tanh)
+
+        ident = sb.tile([P, P], F32, name="ident")
+        ones = sb.tile([P, P], F32, name="ones")
+        quad_base = sb.tile([P, 1], F32, name="quad_base", tag="column")
+        count = sb.tile([P, P], F32, name="count", align_bytes=64)
+        in_quad = sb.tile([P, 32], F32, name="in_quad", align_bytes=64)
+        nc.gpsimd.memset(ones[:], 1.0)
+        for quad in range(4):
+            nc.gpsimd.memset(quad_base[32 * quad : 32 * (quad + 1), :], 32.0 * quad)
+        nc.vector.tensor_tensor_scan(count[:], ones[:], ones[:], 0.0, ALU.mult, ALU.add)
+        nc.vector.transpose(in_quad[:], count[:, 0:32])
+        nc.vector.tensor_scalar(ident[:], count[:], quad_base[:], in_quad[:, 0:1], ALU.subtract, ALU.is_equal)
+        steep_col = sb.tile([P, 1], F32, name="steep_col", tag="column")
+        nc.sync.dma_start(steep_col[:], steep)
+        m_bank = ps.tile([P, PACK, P], F32, name="m_bank")
+        for j in range(PACK):
+            nc.tensor.transpose(m_bank[:, j, :], m_cols[:, j : j + 1].to_broadcast([P, P]), ident[:])
+        lead = sb.tile([P, I], F32, name="lead")
+        nc.scalar.copy(lead[:].rearrange("q (p j) -> q p j", j=PACK), m_bank[:].rearrange("q j p -> q p j"))
+        half_steep = sb.tile([P, 1], F32, name="half_steep")
+        nc.scalar.mul(half_steep[:], steep_col[:], 0.5)
+
+        q_bf = sb.tile([P, Q, PACK], BF16, name="q_bf", align_bytes=64)
+        q_codes = sb.tile([P, Q], U32, name="q_codes", align_bytes=64)
+        q_scales = sb.tile([P, Q], U8, name="q_scales", align_bytes=64)
+        nc.vector.tensor_copy(q_bf[:], q_raw[:].rearrange("p j q -> p q j"))
+        nc.vector.quantize_mx(
+            out=q_codes[:].bitcast(FP8X4), scales=q_scales[:], in_=q_bf[:].rearrange("p q j -> p (q j)")
+        )
+
+        k_scales = sb.tile([P, I], U8, name="k_scales", align_bytes=64)
+        nc.vector.tensor_copy(k_scales[:], scales[:].indirect(offsets[:]))
+
+        banks = []
+        for h in range(2):
+            k_codes = sb.tile([P, HALF], U32, name="k_codes%d" % h, align_bytes=64)
+            nc.vector.tensor_copy(k_codes[:], words[:].bitcast(U32).indirect(offsets[:, 16 * h : 16 * (h + 1)]))
+            bank = ps.tile([P, HALF], F32, name="bank%d" % h)
+            nc.tensor.matmul_mx(
+                out=bank[:],
+                lhsT=q_codes[:].bitcast(FP8X4),
+                lhsT_scale=q_scales[:],
+                rhs=k_codes[:].bitcast(FP8X4),
+                rhs_scale=k_scales[:, h * HALF : (h + 1) * HALF],
+                start=True,
+                stop=True,
+            )
+            banks.append(bank)
+
+        for h in range(2):
+            lo, hi = h * HALF + 1, min((h + 1) * HALF + 1, I)
+            nc.vector.tensor_tensor(lead[:, lo:hi], lead[:, lo:hi], banks[h][:, : hi - lo], ALU.subtract)
+
+        gap = sb.tile([P, I], F32, name="gap")
+        th = sb.tile([P, I], F32, name="th")
+        mag = sb.tile([P, I], F32, name="mag")
+        pos = sb.tile([P, I], F32, name="pos")
+        lg = sb.tile([P, I], F32, name="lg")
+        res = sb.tile([P, I], F32, name="res")
+        for lo, hi in ((0, 256), (256, 384), (384, 512)):
+            h = lo // HALF
+            nc.vector.tensor_tensor(gap[:, lo:hi], banks[h][:, lo - h * HALF : hi - h * HALF], lead[:, lo:hi], ALU.add)
+            nc.scalar.activation(th[:, lo:hi], gap[:, lo:hi], ACT.Tanh, scale=half_steep[:])
+        for h in range(2):
+            cols = slice(h * HALF, (h + 1) * HALF)
+            nc.vector.scalar_tensor_tensor(mag[:, cols], th[:, cols], -1.0, th[:, cols], ALU.mult, ALU.max)
+            nc.vector.tensor_scalar(pos[:, cols], gap[:, cols], steep_col[:], 0.0, ALU.mult, ALU.max)
+        for lo, hi in ((0, 256), (256, 384), (384, 512)):
+            nc.scalar.activation(lg[:, lo:hi], mag[:, lo:hi], ACT.Ln, bias=half[:], scale=0.5)
+            nc.vector.tensor_tensor(res[:, lo:hi], pos[:, lo:hi], lg[:, lo:hi], ALU.subtract)
+            nc.sync.dma_start(out[:, lo:hi], res[:, lo:hi])

@@ -18,6 +18,7 @@ ACT = mybir.ActivationFunctionType
 P = 128
 PACK = 4
 HALF = I // 2
+PIECE = 128
 
 
 def tile_attend_rankgaps_kernel(tc, query, keys_words, keys_scales, margin, steep, offs, out):
@@ -37,11 +38,11 @@ def tile_attend_rankgaps_kernel(tc, query, keys_words, keys_scales, margin, stee
         nc.vector.memset(scales[:].bitcast(I32), 0)
         nc.vector.memset(half[:], 0.5)
 
-        nc.sync.dma_start(offsets[:], offs)
         nc.sync.dma_start(q_raw[:], query.rearrange("(p j) q -> p j q", j=PACK))
+        nc.sync.dma_start(offsets[:], offs)
         nc.scalar.dma_start(m_cols[:], margin.rearrange("o (p j) -> (o p) j", j=PACK))
         for quad in range(4):
-            nc.sync.dma_start(
+            (nc.scalar if quad % 2 else nc.sync).dma_start(
                 scales[32 * quad : 32 * quad + 4, :].bitcast(I32),
                 keys_scales[0][4 * quad : 4 * quad + 4, :].bitcast(I32),
             )
@@ -96,25 +97,22 @@ def tile_attend_rankgaps_kernel(tc, query, keys_words, keys_scales, margin, stee
             )
             banks.append(bank)
 
-        for h in range(2):
-            lo, hi = h * HALF + 1, min((h + 1) * HALF + 1, I)
-            nc.vector.tensor_tensor(lead[:, lo:hi], lead[:, lo:hi], banks[h][:, : hi - lo], ALU.subtract)
-
         gap = sb.tile([P, I], F32, name="gap")
         th = sb.tile([P, I], F32, name="th")
         mag = sb.tile([P, I], F32, name="mag")
         pos = sb.tile([P, I], F32, name="pos")
         lg = sb.tile([P, I], F32, name="lg")
         res = sb.tile([P, I], F32, name="res")
-        for lo, hi in ((0, 256), (256, 384), (384, 512)):
-            h = lo // HALF
-            nc.vector.tensor_tensor(gap[:, lo:hi], banks[h][:, lo - h * HALF : hi - h * HALF], lead[:, lo:hi], ALU.add)
-            nc.scalar.activation(th[:, lo:hi], gap[:, lo:hi], ACT.Tanh, scale=half_steep[:])
         for h in range(2):
-            cols = slice(h * HALF, (h + 1) * HALF)
-            nc.vector.scalar_tensor_tensor(mag[:, cols], th[:, cols], -1.0, th[:, cols], ALU.mult, ALU.max)
-            nc.vector.tensor_scalar(pos[:, cols], gap[:, cols], steep_col[:], 0.0, ALU.mult, ALU.max)
-        for lo, hi in ((0, 256), (256, 384), (384, 512)):
+            lo, hi = h * HALF + 1, min((h + 1) * HALF + 1, I)
+            nc.vector.tensor_tensor(lead[:, lo:hi], lead[:, lo:hi], banks[h][:, : hi - lo], ALU.subtract)
+            for lo in range(h * HALF, (h + 1) * HALF, PIECE):
+                hi = lo + PIECE
+                nc.vector.tensor_tensor(gap[:, lo:hi], banks[h][:, lo - h * HALF : hi - h * HALF], lead[:, lo:hi], ALU.add)
+                nc.scalar.activation(th[:, lo:hi], gap[:, lo:hi], ACT.Tanh, scale=half_steep[:])
+        nc.vector.scalar_tensor_tensor(mag[:], th[:], -1.0, th[:], ALU.mult, ALU.max)
+        nc.vector.tensor_scalar(pos[:], gap[:], steep_col[:], 0.0, ALU.mult, ALU.max)
+        for lo, hi in ((0, 128), (128, 256), (256, 384), (384, 512)):
             nc.scalar.activation(lg[:, lo:hi], mag[:, lo:hi], ACT.Ln, bias=half[:], scale=0.5)
             nc.vector.tensor_tensor(res[:, lo:hi], pos[:, lo:hi], lg[:, lo:hi], ALU.subtract)
             nc.sync.dma_start(out[:, lo:hi], res[:, lo:hi])

@@ -35,18 +35,15 @@ def tile_attend_rankgaps_kernel(tc, query, keys_words, keys_scales, margin, stee
         half = sb.tile([P, 1], F32, name="half")
         warm = sb.tile([P, 1], F32, name="warm")
 
-        nc.vector.memset(scales[:].bitcast(I32), 0)
+        nc.vector.memset(scales[:, : T // 2].bitcast(I32), 0)
+        nc.gpsimd.memset(scales[:, T // 2 :].bitcast(I32), 0)
         nc.vector.memset(half[:], 0.5)
 
-        nc.sync.dma_start(q_raw[:], query.rearrange("(p j) q -> p j q", j=PACK))
         nc.sync.dma_start(offsets[:], offs)
-        nc.scalar.dma_start(m_cols[:], margin.rearrange("o (p j) -> (o p) j", j=PACK))
-        for quad in range(4):
-            (nc.scalar if quad % 2 else nc.sync).dma_start(
-                scales[32 * quad : 32 * quad + 4, :].bitcast(I32),
-                keys_scales[0][4 * quad : 4 * quad + 4, :].bitcast(I32),
-            )
+        nc.scalar.dma_start(q_raw[:], query.rearrange("(p j) q -> p j q", j=PACK))
+        nc.sync.dma_start(scales[0:P:8, :].bitcast(I32), keys_scales[0].bitcast(I32))
         nc.sync.dma_start(words[:], keys_words[0].rearrange("p n t -> p (n t)").bitcast(I32))
+        nc.scalar.dma_start(m_cols[:], margin.rearrange("o (p j) -> (o p) j", j=PACK))
         nc.scalar.activation(warm[:], half[:], ACT.Tanh)
 
         ident = sb.tile([P, P], F32, name="ident")
@@ -70,16 +67,23 @@ def tile_attend_rankgaps_kernel(tc, query, keys_words, keys_scales, margin, stee
         half_steep = sb.tile([P, 1], F32, name="half_steep")
         nc.scalar.mul(half_steep[:], steep_col[:], 0.5)
 
+        picked = sb.tile([P, I], U8, name="picked", align_bytes=64)
+        k_scales = sb.tile([P, I], U8, name="k_scales", align_bytes=64)
+        nc.vector.tensor_copy(picked[:], scales[:].indirect(offsets[:]))
+        for quad in range(4):
+            (nc.scalar if quad % 2 else nc.sync).dma_start(
+                k_scales[32 * quad : 32 * quad + 4, :].bitcast(I32),
+                picked[32 * quad : 32 * (quad + 1) : 8, :].bitcast(I32),
+            )
+
         q_bf = sb.tile([P, Q, PACK], BF16, name="q_bf", align_bytes=64)
         q_codes = sb.tile([P, Q], U32, name="q_codes", align_bytes=64)
         q_scales = sb.tile([P, Q], U8, name="q_scales", align_bytes=64)
-        nc.vector.tensor_copy(q_bf[:], q_raw[:].rearrange("p j q -> p q j"))
+        nc.scalar.copy(q_bf[:], q_raw[:].rearrange("p j q -> p q j"))
         nc.vector.quantize_mx(
             out=q_codes[:].bitcast(FP8X4), scales=q_scales[:], in_=q_bf[:].rearrange("p q j -> p (q j)")
         )
 
-        k_scales = sb.tile([P, I], U8, name="k_scales", align_bytes=64)
-        nc.vector.tensor_copy(k_scales[:], scales[:].indirect(offsets[:]))
 
         banks = []
         for h in range(2):

@@ -41,7 +41,7 @@ def tile_attend_rankgaps_kernel(tc, query, keys_words, keys_scales, margin, stee
 
         nc.sync.dma_start(offsets[:], offs)
         nc.scalar.dma_start(q_raw[:], query.rearrange("(p j) q -> p j q", j=PACK))
-        nc.sync.dma_start(scales[0:P:8, :].bitcast(I32), keys_scales[0].bitcast(I32))
+        nc.sync.dma_start(scales[0:16, :].bitcast(I32), keys_scales[0].bitcast(I32))
         nc.sync.dma_start(words[:], keys_words[0].rearrange("p n t -> p (n t)").bitcast(I32))
         nc.scalar.dma_start(m_cols[:], margin.rearrange("o (p j) -> (o p) j", j=PACK))
         nc.scalar.activation(warm[:], half[:], ACT.Tanh)
@@ -69,12 +69,15 @@ def tile_attend_rankgaps_kernel(tc, query, keys_words, keys_scales, margin, stee
 
         picked = sb.tile([P, I], U8, name="picked", align_bytes=64)
         k_scales = sb.tile([P, I], U8, name="k_scales", align_bytes=64)
-        nc.vector.tensor_copy(picked[:], scales[:].indirect(offsets[:]))
-        for quad in range(4):
-            (nc.scalar if quad % 2 else nc.sync).dma_start(
-                k_scales[32 * quad : 32 * quad + 4, :].bitcast(I32),
-                picked[32 * quad : 32 * (quad + 1) : 8, :].bitcast(I32),
-            )
+        for h in range(2):
+            cols = slice(h * HALF, (h + 1) * HALF)
+            nc.vector.tensor_copy(picked[:, cols], scales[:].indirect(offsets[:, 16 * h : 16 * (h + 1)]))
+            for quad in range(1, 4):
+                (nc.sync if quad % 2 else nc.scalar).dma_start(
+                    k_scales[32 * quad : 32 * quad + 4, cols].bitcast(I32),
+                    picked[4 * quad : 4 * quad + 4, cols].bitcast(I32),
+                )
+        nc.vector.tensor_copy(k_scales[0:4, :].bitcast(I32), picked[0:4, :].bitcast(I32))
 
         q_bf = sb.tile([P, Q, PACK], BF16, name="q_bf", align_bytes=64)
         q_codes = sb.tile([P, Q], U32, name="q_codes", align_bytes=64)

@@ -17,7 +17,12 @@ ACT = mybir.ActivationFunctionType
 
 P = 128
 PACK = 4
+QUAD = 32
+QUADS = P // QUAD
+BLOCKS = D // 32
+ROWS = BLOCKS // QUADS
 HALF = I // 2
+LIST_COLS = HALF // 16
 PIECE = 128
 
 
@@ -32,33 +37,33 @@ def tile_attend_rankgaps_kernel(tc, query, keys_words, keys_scales, margin, stee
         words = sb.tile([P, T], I32, name="words", align_bytes=64)
         scales = sb.tile([P, T], U8, name="scales", align_bytes=64)
         m_cols = sb.tile([P, PACK], F32, name="m_cols")
-        half = sb.tile([P, 1], F32, name="half")
-        warm = sb.tile([P, 1], F32, name="warm")
+        ln_bias = sb.tile([P, 1], F32, name="half")
 
         nc.vector.memset(scales[:, : T // 2].bitcast(I32), 0)
         nc.gpsimd.memset(scales[:, T // 2 :].bitcast(I32), 0)
-        nc.vector.memset(half[:], 0.5)
+        nc.vector.memset(ln_bias[:], 0.5)
 
         nc.sync.dma_start(offsets[:], offs)
         nc.scalar.dma_start(q_raw[:], query.rearrange("(p j) q -> p j q", j=PACK))
-        nc.sync.dma_start(scales[0:16, :].bitcast(I32), keys_scales[0].bitcast(I32))
+        nc.sync.dma_start(scales[0:BLOCKS, :].bitcast(I32), keys_scales[0].bitcast(I32))
         nc.sync.dma_start(words[:], keys_words[0].rearrange("p n t -> p (n t)").bitcast(I32))
         nc.scalar.dma_start(m_cols[:], margin.rearrange("o (p j) -> (o p) j", j=PACK))
-        nc.scalar.activation(warm[:], half[:], ACT.Tanh)
 
         ident = sb.tile([P, P], F32, name="ident")
         ones = sb.tile([P, P], F32, name="ones")
         quad_base = sb.tile([P, 1], F32, name="quad_base", tag="column")
         count = sb.tile([P, P], F32, name="count", align_bytes=64)
-        in_quad = sb.tile([P, 32], F32, name="in_quad", align_bytes=64)
+        in_quad = sb.tile([P, QUAD], F32, name="in_quad", align_bytes=64)
         nc.gpsimd.memset(ones[:], 1.0)
-        for quad in range(4):
-            nc.gpsimd.memset(quad_base[32 * quad : 32 * (quad + 1), :], 32.0 * quad)
+        for quad in range(QUADS):
+            nc.gpsimd.memset(quad_base[QUAD * quad : QUAD * (quad + 1), :], float(QUAD * quad))
         nc.vector.tensor_tensor_scan(count[:], ones[:], ones[:], 0.0, ALU.mult, ALU.add)
-        nc.vector.transpose(in_quad[:], count[:, 0:32])
+        nc.vector.transpose(in_quad[:], count[:, 0:QUAD])
         nc.vector.tensor_scalar(ident[:], count[:], quad_base[:], in_quad[:, 0:1], ALU.subtract, ALU.is_equal)
+
         steep_col = sb.tile([P, 1], F32, name="steep_col", tag="column")
         nc.sync.dma_start(steep_col[:], steep)
+
         m_bank = ps.tile([P, PACK, P], F32, name="m_bank")
         for j in range(PACK):
             nc.tensor.transpose(m_bank[:, j, :], m_cols[:, j : j + 1].to_broadcast([P, P]), ident[:])
@@ -71,13 +76,15 @@ def tile_attend_rankgaps_kernel(tc, query, keys_words, keys_scales, margin, stee
         k_scales = sb.tile([P, I], U8, name="k_scales", align_bytes=64)
         for h in range(2):
             cols = slice(h * HALF, (h + 1) * HALF)
-            nc.vector.tensor_copy(picked[:, cols], scales[:].indirect(offsets[:, 16 * h : 16 * (h + 1)]))
-            for quad in range(1, 4):
-                (nc.sync if quad % 2 else nc.scalar).dma_start(
-                    k_scales[32 * quad : 32 * quad + 4, cols].bitcast(I32),
-                    picked[4 * quad : 4 * quad + 4, cols].bitcast(I32),
+            listed = offsets[:, LIST_COLS * h : LIST_COLS * (h + 1)]
+            nc.vector.tensor_copy(picked[:, cols], scales[:].indirect(listed))
+            for quad in range(1, QUADS):
+                queue = nc.sync if quad % 2 else nc.scalar
+                queue.dma_start(
+                    k_scales[QUAD * quad : QUAD * quad + ROWS, cols].bitcast(I32),
+                    picked[ROWS * quad : ROWS * (quad + 1), cols].bitcast(I32),
                 )
-        nc.vector.tensor_copy(k_scales[0:4, :].bitcast(I32), picked[0:4, :].bitcast(I32))
+        nc.vector.tensor_copy(k_scales[0:ROWS, :].bitcast(I32), picked[0:ROWS, :].bitcast(I32))
 
         q_bf = sb.tile([P, Q, PACK], BF16, name="q_bf", align_bytes=64)
         q_codes = sb.tile([P, Q], U32, name="q_codes", align_bytes=64)
@@ -87,11 +94,11 @@ def tile_attend_rankgaps_kernel(tc, query, keys_words, keys_scales, margin, stee
             out=q_codes[:].bitcast(FP8X4), scales=q_scales[:], in_=q_bf[:].rearrange("p q j -> p (q j)")
         )
 
-
         banks = []
         for h in range(2):
             k_codes = sb.tile([P, HALF], U32, name="k_codes%d" % h, align_bytes=64)
-            nc.vector.tensor_copy(k_codes[:], words[:].bitcast(U32).indirect(offsets[:, 16 * h : 16 * (h + 1)]))
+            listed = offsets[:, LIST_COLS * h : LIST_COLS * (h + 1)]
+            nc.vector.tensor_copy(k_codes[:], words[:].bitcast(U32).indirect(listed))
             bank = ps.tile([P, HALF], F32, name="bank%d" % h)
             nc.tensor.matmul_mx(
                 out=bank[:],
@@ -105,21 +112,25 @@ def tile_attend_rankgaps_kernel(tc, query, keys_words, keys_scales, margin, stee
             banks.append(bank)
 
         gap = sb.tile([P, I], F32, name="gap")
-        th = sb.tile([P, I], F32, name="th")
-        mag = sb.tile([P, I], F32, name="mag")
-        pos = sb.tile([P, I], F32, name="pos")
-        lg = sb.tile([P, I], F32, name="lg")
-        res = sb.tile([P, I], F32, name="res")
+        tanh_half = sb.tile([P, I], F32, name="th")
+        tanh_abs = sb.tile([P, I], F32, name="mag")
+        relu_x = sb.tile([P, I], F32, name="pos")
+        log_part = sb.tile([P, I], F32, name="lg")
+        result = sb.tile([P, I], F32, name="res")
         for h in range(2):
-            lo, hi = h * HALF + 1, min((h + 1) * HALF + 1, I)
-            nc.vector.tensor_tensor(lead[:, lo:hi], lead[:, lo:hi], banks[h][:, : hi - lo], ALU.subtract)
-            for lo in range(h * HALF, (h + 1) * HALF, PIECE):
-                hi = lo + PIECE
-                nc.vector.tensor_tensor(gap[:, lo:hi], banks[h][:, lo - h * HALF : hi - h * HALF], lead[:, lo:hi], ALU.add)
-                nc.scalar.activation(th[:, lo:hi], gap[:, lo:hi], ACT.Tanh, scale=half_steep[:])
-        nc.vector.scalar_tensor_tensor(mag[:], th[:], -1.0, th[:], ALU.mult, ALU.max)
-        nc.vector.tensor_scalar(pos[:], gap[:], steep_col[:], 0.0, ALU.mult, ALU.max)
-        for lo, hi in ((0, 128), (128, 256), (256, 384), (384, 512)):
-            nc.scalar.activation(lg[:, lo:hi], mag[:, lo:hi], ACT.Ln, bias=half[:], scale=0.5)
-            nc.vector.tensor_tensor(res[:, lo:hi], pos[:, lo:hi], lg[:, lo:hi], ALU.subtract)
-            nc.sync.dma_start(out[:, lo:hi], res[:, lo:hi])
+            first = h * HALF
+            shifted = slice(first + 1, min(first + HALF + 1, I))
+            width = shifted.stop - shifted.start
+            nc.vector.tensor_tensor(lead[:, shifted], lead[:, shifted], banks[h][:, :width], ALU.subtract)
+            for at in range(0, HALF, PIECE):
+                cols = slice(first + at, first + at + PIECE)
+                nc.vector.tensor_tensor(gap[:, cols], banks[h][:, at : at + PIECE], lead[:, cols], ALU.add)
+                nc.scalar.activation(tanh_half[:, cols], gap[:, cols], ACT.Tanh, scale=half_steep[:])
+
+        nc.vector.scalar_tensor_tensor(tanh_abs[:], tanh_half[:], -1.0, tanh_half[:], ALU.mult, ALU.max)
+        nc.vector.tensor_scalar(relu_x[:], gap[:], steep_col[:], 0.0, ALU.mult, ALU.max)
+        for at in range(0, I, PIECE):
+            cols = slice(at, at + PIECE)
+            nc.scalar.activation(log_part[:, cols], tanh_abs[:, cols], ACT.Ln, bias=ln_bias[:], scale=0.5)
+            nc.vector.tensor_tensor(result[:, cols], relu_x[:, cols], log_part[:, cols], ALU.subtract)
+            nc.sync.dma_start(out[:, cols], result[:, cols])

from contextlib import ExitStack

import concourse.mybir as mybir

D, T, I, Q = 512, 2048, 512, 128
FLOPS = 2 * D * I * Q

F32 = mybir.dt.float32
BF16 = mybir.dt.bfloat16
I32 = mybir.dt.int32
U32 = mybir.dt.uint32
U16 = mybir.dt.uint16
U8 = mybir.dt.uint8
FP8X4 = mybir.dt.float8_e4m3fn_x4
ALU = mybir.AluOpType
ACT = mybir.ActivationFunctionType

P = 128
PACK = 4
QUAD = 32
QUADS = P // QUAD
BLOCKS = D // 32
ROWS = BLOCKS // QUADS
HALF = I // 2
LIST_COLS = HALF // 16
PIECE = 128


def tile_attend_rankgaps_kernel(tc, query, keys_words, keys_scales, margin, steep, offs, out):
    nc = tc.nc
    with ExitStack() as ctx:
        sb = ctx.enter_context(tc.tile_pool(name="sb", bufs=1))
        ps = ctx.enter_context(tc.psum_pool(name="ps", bufs=1))

        offsets = sb.tile([P, I // 16], U16, name="offsets")
        q_raw = sb.tile([P, PACK, Q], F32, name="q_raw")
        words = sb.tile([P, T], I32, name="words", align_bytes=64)
        scales = sb.tile([P, T], U8, name="scales", align_bytes=64)
        m_cols = sb.tile([P, PACK], F32, name="m_cols")
        ln_bias = sb.tile([P, 1], F32, name="half")

        nc.vector.memset(scales[:, : T // 2].bitcast(I32), 0)
        nc.gpsimd.memset(scales[:, T // 2 :].bitcast(I32), 0)
        nc.vector.memset(ln_bias[:], 0.5)

        nc.sync.dma_start(offsets[:], offs)
        nc.scalar.dma_start(q_raw[:], query.rearrange("(p j) q -> p j q", j=PACK))
        nc.sync.dma_start(scales[0:BLOCKS, :].bitcast(I32), keys_scales[0].bitcast(I32))
        nc.sync.dma_start(words[:], keys_words[0].rearrange("p n t -> p (n t)").bitcast(I32))
        nc.scalar.dma_start(m_cols[:], margin.rearrange("o (p j) -> (o p) j", j=PACK))

        ident = sb.tile([P, P], F32, name="ident")
        ones = sb.tile([P, P], F32, name="ones")
        quad_base = sb.tile([P, 1], F32, name="quad_base", tag="column")
        count = sb.tile([P, P], F32, name="count", align_bytes=64)
        in_quad = sb.tile([P, QUAD], F32, name="in_quad", align_bytes=64)
        nc.gpsimd.memset(ones[:], 1.0)
        for quad in range(QUADS):
            nc.gpsimd.memset(quad_base[QUAD * quad : QUAD * (quad + 1), :], float(QUAD * quad))
        nc.vector.tensor_tensor_scan(count[:], ones[:], ones[:], 0.0, ALU.mult, ALU.add)
        nc.vector.transpose(in_quad[:], count[:, 0:QUAD])
        nc.vector.tensor_scalar(ident[:], count[:], quad_base[:], in_quad[:, 0:1], ALU.subtract, ALU.is_equal)

        steep_col = sb.tile([P, 1], F32, name="steep_col", tag="column")
        nc.sync.dma_start(steep_col[:], steep)

        m_bank = ps.tile([P, PACK, P], F32, name="m_bank")
        for j in range(PACK):
            nc.tensor.transpose(m_bank[:, j, :], m_cols[:, j : j + 1].to_broadcast([P, P]), ident[:])
        lead = sb.tile([P, I], F32, name="lead")
        nc.scalar.copy(lead[:].rearrange("q (p j) -> q p j", j=PACK), m_bank[:].rearrange("q j p -> q p j"))
        half_steep = sb.tile([P, 1], F32, name="half_steep")
        nc.scalar.mul(half_steep[:], steep_col[:], 0.5)

        picked = sb.tile([P, I], U8, name="picked", align_bytes=64)
        k_scales = sb.tile([P, I], U8, name="k_scales", align_bytes=64)
        for h in range(2):
            cols = slice(h * HALF, (h + 1) * HALF)
            listed = offsets[:, LIST_COLS * h : LIST_COLS * (h + 1)]
            nc.vector.tensor_copy(picked[:, cols], scales[:].indirect(listed))
            for quad in range(1, QUADS):
                queue = nc.sync if quad % 2 else nc.scalar
                queue.dma_start(
                    k_scales[QUAD * quad : QUAD * quad + ROWS, cols].bitcast(I32),
                    picked[ROWS * quad : ROWS * (quad + 1), cols].bitcast(I32),
                )
        nc.vector.tensor_copy(k_scales[0:ROWS, :].bitcast(I32), picked[0:ROWS, :].bitcast(I32))

        q_bf = sb.tile([P, Q, PACK], BF16, name="q_bf", align_bytes=64)
        q_codes = sb.tile([P, Q], U32, name="q_codes", align_bytes=64)
        q_scales = sb.tile([P, Q], U8, name="q_scales", align_bytes=64)
        nc.scalar.copy(q_bf[:], q_raw[:].rearrange("p j q -> p q j"))
        nc.vector.quantize_mx(
            out=q_codes[:].bitcast(FP8X4), scales=q_scales[:], in_=q_bf[:].rearrange("p q j -> p (q j)")
        )

        banks = []
        for h in range(2):
            k_codes = sb.tile([P, HALF], U32, name="k_codes%d" % h, align_bytes=64)
            listed = offsets[:, LIST_COLS * h : LIST_COLS * (h + 1)]
            nc.vector.tensor_copy(k_codes[:], words[:].bitcast(U32).indirect(listed))
            bank = ps.tile([P, HALF], F32, name="bank%d" % h)
            nc.tensor.matmul_mx(
                out=bank[:],
                lhsT=q_codes[:].bitcast(FP8X4),
                lhsT_scale=q_scales[:],
                rhs=k_codes[:].bitcast(FP8X4),
                rhs_scale=k_scales[:, h * HALF : (h + 1) * HALF],
                start=True,
                stop=True,
            )
            banks.append(bank)

        gap = sb.tile([P, I], F32, name="gap")
        tanh_half = sb.tile([P, I], F32, name="th")
        tanh_abs = sb.tile([P, I], F32, name="mag")
        relu_x = sb.tile([P, I], F32, name="pos")
        log_part = sb.tile([P, I], F32, name="lg")
        result = sb.tile([P, I], F32, name="res")
        for h in range(2):
            first = h * HALF
            shifted = slice(first + 1, min(first + HALF + 1, I))
            width = shifted.stop - shifted.start
            nc.vector.tensor_tensor(lead[:, shifted], lead[:, shifted], banks[h][:, :width], ALU.subtract)
            for at in range(0, HALF, PIECE):
                cols = slice(first + at, first + at + PIECE)
                nc.vector.tensor_tensor(gap[:, cols], banks[h][:, at : at + PIECE], lead[:, cols], ALU.add)
                nc.scalar.activation(tanh_half[:, cols], gap[:, cols], ACT.Tanh, scale=half_steep[:])

        nc.vector.scalar_tensor_tensor(tanh_abs[:], tanh_half[:], -1.0, tanh_half[:], ALU.mult, ALU.max)
        nc.vector.tensor_scalar(relu_x[:], gap[:], steep_col[:], 0.0, ALU.mult, ALU.max)
        for at in range(0, I, PIECE):
            cols = slice(at, at + PIECE)
            nc.scalar.activation(log_part[:, cols], tanh_abs[:, cols], ACT.Ln, bias=ln_bias[:], scale=0.5)
            nc.vector.tensor_tensor(result[:, cols], relu_x[:, cols], log_part[:, cols], ALU.subtract)
            nc.sync.dma_start(out[:, cols], result[:, cols])
